import numpy as np
import ml_dtypes


def mxq(x, axis, fmt="e4m3"):
    dtype, down = {"e4m3": (ml_dtypes.float8_e4m3fn, 7), "e5m2": (ml_dtypes.float8_e5m2, 14)}[fmt]
    v = np.moveaxis(np.asarray(x, np.float32).astype(ml_dtypes.bfloat16).astype(np.float64), axis, -1)
    blocks = v.reshape(v.shape[:-1] + (-1, 32))
    amax = np.abs(blocks).max(-1, keepdims=True)
    byte = np.maximum(np.where(amax > 0, np.frexp(amax)[1] - 1 + 127, 0) - down, 1)
    scale = np.exp2(byte - 127.0)
    codes = (blocks / scale).astype(np.float32).astype(dtype).astype(np.float64)
    return np.moveaxis((codes * scale).reshape(v.shape), -1, axis)


WIDE = False


def mx_kscale(k):
    if not WIDE:
        return np.ones(k)
    levels = np.array([10, -10, 5, -5, 0])
    if k % 512:
        return np.exp2(np.random.permutation(np.resize(levels, k // 32))).repeat(32)
    a = np.empty((k // 512, 16))
    for p in range(k // 512):
        a[p, :8] = np.random.permutation(np.resize(levels, 8))
        for g in range(8):
            far = levels[np.abs(levels - a[p, g]) >= 10]
            a[p, g + 8] = far[np.random.randint(len(far))]
    return np.exp2(a.ravel()).repeat(32)


def f64(x):
    return np.asarray(x).astype(np.float64)


def striped(idx):
    return np.tile(idx.reshape(-1, 16).T, (8, 1)).astype(np.uint16)


def unstriped(offs):
    return offs[:16].T.reshape(-1).astype(np.int64)


def pack_weight(w):
    k, n = w.shape
    w = f64(np.asarray(w, np.float32).astype(ml_dtypes.bfloat16)).reshape(k // 32, 32, n)
    amax = np.abs(w).max(1)
    byte = np.clip(np.where(amax > 0, np.frexp(amax)[1] - 1 + 127 - 7, 1), 1, 254)
    scaled = (w * np.exp2(127.0 - byte)[:, None, :]).reshape(k, n).astype(np.float32)
    words = np.ascontiguousarray(scaled.reshape(k // 512, 128, 4, n).transpose(0, 1, 3, 2)).astype(ml_dtypes.float8_e4m3fn).view(np.uint8)
    return words, np.ascontiguousarray(byte.astype(np.uint8).reshape(k // 512, 16, n))


def unpack_weight(words, scales):
    g, p, n, _ = words.shape
    vals = np.ascontiguousarray(words).view(ml_dtypes.float8_e4m3fn).astype(np.float64) * np.repeat(np.exp2(scales.astype(np.float64) - 127.0), 8, axis=1)[..., None]
    return vals.transpose(0, 1, 3, 2).reshape(g * 512, n)


K, T, S, D, N, V = 512, 2048, 1024, 4, 128, 256
P = 2 ** 7


def setup_inputs():
    n = np.random.standard_normal
    s = mx_kscale(K)[:, None]
    packed_xT = pack_weight(n((K, T)) * s)
    return {
        "x_words": packed_xT[0],
        "x_scales": packed_xT[1],
        "w1": (n((K, N)) / np.sqrt(K) / s).astype(np.float32),
        "pred": (0.7 * n((N, V))).astype(np.float32),
        "inns": (np.random.uniform(0.5, 2.0, (N, V))).astype(np.float32),
        "miss": (np.tile(np.random.uniform(0.2, 0.9, V), (P, 1))).astype(np.float32),
        "gain": (np.tile(np.random.uniform(0.2, 0.9, V), (P, 1))).astype(np.float32),
        "offs": striped(np.random.permutation(T)[:S]),
    }


def reference(x_words, x_scales, w1, pred, inns, miss, gain, offs):
    xq = unpack_weight(x_words, x_scales)[:, unstriped(offs)]
    y = mxq(f64(w1), 0, "e4m3").T @ xq
    nu = y - (np.repeat(f64(pred), D, axis=1))
    lik = np.exp(-0.5 * (((nu) ** 2) / (np.repeat(f64(inns), D, axis=1))))
    tot = lik.reshape(len(lik), -1, D).sum(axis=2) + f64(miss)[:1]
    beta = lik / np.repeat(tot, D, axis=1)
    b2 = beta * ((nu) ** 2)
    bn = beta * nu
    comb = bn.reshape(len(bn), -1, D).sum(axis=2)
    return (-1.0 * (f64(gain)[:1] * (-1.0 * (f64(miss)[:1] / tot) + 1.0)) + 1.0) * f64(inns) + ((f64(gain)[:1]) ** 2) * (b2.reshape(len(b2), -1, D).sum(axis=2) - ((comb) ** 2))

@@ -1,0 +1,151 @@
+from contextlib import ExitStack
+
+import concourse.mybir as mybir
+from concourse.masks import make_identity
+
+K, T, S, D, N, V = 512, 2048, 1024, 4, 128, 256
+FLOPS = 2 * K * N * S
+
+F32 = mybir.dt.float32
+BF16 = mybir.dt.bfloat16
+I32 = mybir.dt.int32
+U32 = mybir.dt.uint32
+U16 = mybir.dt.uint16
+U8 = mybir.dt.uint8
+FP8X4 = mybir.dt.float8_e4m3fn_x4
+ACT = mybir.ActivationFunctionType
+ALU = mybir.AluOpType
+
+P = 128
+PACK = 4
+BLOCKS = V // P
+CH = 256
+CV = CH // D
+
+
+def tile_picked_ypdaf_var_p_kernel(tc, x_words, x_scales, w1, pred, inns, miss, gain, offs, out):
+    nc = tc.nc
+    with ExitStack() as ctx:
+        keep = ctx.enter_context(tc.tile_pool(name="keep", bufs=1))
+        psum = ctx.enter_context(tc.psum_pool(name="psum", bufs=2))
+
+        offsets = keep.tile([P, S // 16], U16, name="offsets")
+        nc.sync.dma_start(offsets[:], offs)
+
+        inns_sb = keep.tile([P, V], F32, name="inns_sb")
+        nc.scalar.dma_start(out=inns_sb[:], in_=inns)
+        w_raw = keep.tile([P, PACK, N], F32, name="w_raw")
+        nc.scalar.dma_start(out=w_raw[:], in_=w1.rearrange("(p t) n -> p t n", t=PACK))
+        scales = keep.tile([P, T], U8, name="scales", tag="scales", align_bytes=64)
+        nc.vector.memset(scales[:].bitcast(I32), 0)
+        for quad in range(4):
+            nc.sync.dma_start(out=scales[32 * quad : 32 * quad + 4, :].bitcast(I32), in_=x_scales[0, 4 * quad : 4 * quad + 4, :].bitcast(I32))
+        words = keep.tile([P, T], U32, name="words", align_bytes=64)
+        nc.sync.dma_start(out=words[:].bitcast(I32), in_=x_words[0].rearrange("p c t -> p (c t)").bitcast(I32))
+        pred_sb = keep.tile([P, V], F32, name="pred_sb")
+        nc.sync.dma_start(out=pred_sb[:], in_=pred)
+        g_tile = keep.tile([P, BLOCKS], F32, name="g_tile")
+        m_tile = keep.tile([P, BLOCKS], F32, name="m_tile")
+        g_col = g_tile[:]
+        m_col = m_tile[:]
+        with nc.allow_non_contiguous_dma(reason="one value a partition"):
+            nc.sync.dma_start(out=g_col, in_=gain[0].rearrange("(b p) -> p b", p=P))
+            nc.sync.dma_start(out=m_col, in_=miss[0].rearrange("(b p) -> p b", p=P))
+
+        ident = keep.tile([P, P], F32, name="ident")
+        make_identity(nc, ident[:])
+
+        log2inns = keep.tile([P, V], F32, name="log2inns")
+        nc.scalar.activation(log2inns[:], inns_sb[:], ACT.Ln, scale=2.0)
+        w_bf = keep.tile([P, N, PACK], BF16, name="w_bf", align_bytes=64)
+        nc.scalar.copy(out=w_bf[:], in_=w_raw[:].rearrange("p t n -> p n t"))
+        sigma = keep.tile([P, V], F32, name="sigma")
+        nc.scalar.activation(sigma[:], log2inns[:], ACT.Exp, scale=-0.5)
+
+        picked_scales = keep.tile([P, S], U8, name="picked_scales", align_bytes=64)
+        for b in range(BLOCKS):
+            nc.vector.tensor_copy(picked_scales[:, b * 512 : (b + 1) * 512], scales[:].indirect(offsets[:, b * 32 : (b + 1) * 32]))
+        w_codes = keep.tile([P, N], U32, name="w_codes", tag="scales", align_bytes=64)
+        w_scales = keep.tile([P, N], U8, name="w_scales", align_bytes=64)
+        nc.vector.quantize_mx(out=w_codes[:].bitcast(FP8X4), scales=w_scales[:], in_=w_bf[:].rearrange("p n t -> p (n t)"))
+
+        g2 = keep.tile([P, BLOCKS], F32, name="g2")
+        ng2 = keep.tile([P, BLOCKS], F32, name="ng2")
+        gm = keep.tile([P, BLOCKS], F32, name="gm")
+        omg = keep.tile([P, BLOCKS], F32, name="omg")
+        nc.scalar.activation(g2[:], g_col, ACT.Square, scale=2.0**0.5)
+        nc.scalar.activation(ng2[:], g2[:], ACT.Copy, scale=-1.0)
+        nc.scalar.activation(omg[:], g_col, ACT.Identity, scale=-1.0, bias=1.0)
+        for b in range(BLOCKS):
+            nc.scalar.activation(gm[:, b : b + 1], m_col[:, b : b + 1], ACT.Copy, scale=g_col[:, b : b + 1])
+
+        def block_tiles(name):
+            return [keep.tile([P, D, P], F32, name=f"{name}{b}") for b in range(BLOCKS)]
+
+        nu, z, q, lik, e1, e2 = (block_tiles(n) for n in ("nu", "z", "q", "lik", "e1", "e2"))
+
+        ys = []
+
+        def gather(c):
+            picked = keep.tile([P, CH], U32, name=f"picked{c}", align_bytes=64)
+            nc.vector.tensor_copy(picked[:], words[:].indirect(offsets[:, c * 16 : (c + 1) * 16]))
+            y = psum.tile([P, CH], F32, name=f"y{c}", tag="y")
+            nc.tensor.matmul_mx(out=y[:], lhsT=w_codes[:].bitcast(FP8X4), lhsT_scale=w_scales[:],
+                                rhs=picked[:].bitcast(FP8X4), rhs_scale=picked_scales[:, c * CH : (c + 1) * CH], start=True, stop=True)
+            ys.append(y)
+
+        def innov(c):
+            b, h = divmod(c, 2)
+            cols = slice(h * CV, (h + 1) * CV)
+            tr = slice(c * CV, (c + 1) * CV)
+            nc.vector.tensor_tensor(nu[b][:, :, cols], ys[c][:].rearrange("p (v d) -> p d v", d=D),
+                                    pred_sb[:, tr].unsqueeze(1).to_broadcast([P, D, CV]), ALU.subtract)
+            nc.vector.tensor_tensor(z[b][:, :, cols], nu[b][:, :, cols],
+                                    sigma[:, tr].unsqueeze(1).to_broadcast([P, D, CV]), ALU.mult)
+            nc.scalar.activation(q[b][:, :, cols], z[b][:, :, cols], ACT.Square)
+            nc.scalar.activation(lik[b][:, :, cols], q[b][:, :, cols], ACT.Exp, scale=-1.0)
+
+        def sum_over_d(src, name, b):
+            acc = psum.tile([P, P], F32, name=f"{name}{b}", tag=name)
+            for d in range(D):
+                nc.tensor.matmul(acc[:], src[:, d, :], ident[:], start=(d == 0), stop=(d == D - 1), is_transpose=True)
+            return acc
+
+        gather(0)
+        gather(1)
+        innov(0)
+        gather(2)
+        innov(1)
+        gather(3)
+        innov(2)
+        innov(3)
+        z0 = [sum_over_d(lik[b], "z0_", b) for b in range(BLOCKS)]
+        z1, z2 = [], []
+        for b in range(BLOCKS):
+            for dd in range(0, D, 2):
+                nc.vector.tensor_tensor(e2[b][:, dd : dd + 2, :], lik[b][:, dd : dd + 2, :], q[b][:, dd : dd + 2, :], ALU.mult)
+            z2.append(sum_over_d(e2[b], "z2_", b))
+            for dd in range(0, D, 2):
+                nc.vector.tensor_tensor(e1[b][:, dd : dd + 2, :], lik[b][:, dd : dd + 2, :], z[b][:, dd : dd + 2, :], ALU.mult)
+            z1.append(sum_over_d(e1[b], "z1_", b))
+
+        for b in range(BLOCKS):
+            col = slice(b, b + 1)
+            rho = keep.tile([P, P], F32, name=f"rho{b}")
+            nc.scalar.activation(rho[:], z0[b][:], ACT.Abs_reciprocal_sqrt, bias=m_col[:, col])
+            r = keep.tile([P, P], F32, name=f"r{b}")
+            nc.scalar.activation(r[:], rho[:], ACT.Square)
+            k3 = keep.tile([P, P], F32, name=f"k3{b}")
+            nc.scalar.activation(k3[:], r[:], ACT.Identity, scale=gm[:, col], bias=omg[:, col])
+            k = keep.tile([P, P], F32, name=f"k{b}")
+            nc.vector.scalar_tensor_tensor(k[:], z2[b][:], g2[:, col], r[:], ALU.mult, ALU.mult)
+            c1 = keep.tile([P, P], F32, name=f"c1{b}")
+            nc.vector.tensor_tensor(c1[:], z1[b][:], r[:], ALU.mult)
+            c2 = keep.tile([P, P], F32, name=f"c2{b}")
+            nc.vector.scalar_tensor_tensor(c2[:], c1[:], ng2[:, col], c1[:], ALU.mult, ALU.mult)
+            back = psum.tile([P, CH], F32, name=f"back{b}", tag="y")
+            for i, term in enumerate((k3, k, c2)):
+                nc.tensor.matmul(back[:, 0:P], term[:], ident[:], start=(i == 0), stop=(i == 2), is_transpose=True)
+            res = keep.tile([P, P], F32, name=f"res{b}")
+            nc.vector.tensor_tensor(res[:], back[:, 0:P], inns_sb[:, b * P : (b + 1) * P], ALU.mult)
+            nc.sync.dma_start(out=out[:, b * P : (b + 1) * P], in_=res[:])

@@ -32,42 +32,42 @@ def tile_picked_ypdaf_var_p_kernel(tc, x_words, x_scales, w1, pred, inns, miss, 
         offsets = keep.tile([P, S // 16], U16, name="offsets")
         nc.sync.dma_start(offsets[:], offs)
 
+        w_raw = keep.tile([P, PACK, N], F32, name="w_raw", tag="w_raw")
+        nc.sync.dma_start(out=w_raw[:], in_=w1.rearrange("(p t) n -> p t n", t=PACK))
         inns_sb = keep.tile([P, V], F32, name="inns_sb")
-        nc.scalar.dma_start(out=inns_sb[:], in_=inns)
-        w_raw = keep.tile([P, PACK, N], F32, name="w_raw")
-        nc.scalar.dma_start(out=w_raw[:], in_=w1.rearrange("(p t) n -> p t n", t=PACK))
-        scales = keep.tile([P, T], U8, name="scales", tag="scales", align_bytes=64)
+        nc.sync.dma_start(out=inns_sb[:], in_=inns)
+        scales = keep.tile([P, T], U8, name="scales", align_bytes=64)
         nc.vector.memset(scales[:].bitcast(I32), 0)
         for quad in range(4):
             nc.sync.dma_start(out=scales[32 * quad : 32 * quad + 4, :].bitcast(I32), in_=x_scales[0, 4 * quad : 4 * quad + 4, :].bitcast(I32))
         words = keep.tile([P, T], U32, name="words", align_bytes=64)
         nc.sync.dma_start(out=words[:].bitcast(I32), in_=x_words[0].rearrange("p c t -> p (c t)").bitcast(I32))
-        pred_sb = keep.tile([P, V], F32, name="pred_sb")
-        nc.sync.dma_start(out=pred_sb[:], in_=pred)
-        g_tile = keep.tile([P, BLOCKS], F32, name="g_tile")
-        m_tile = keep.tile([P, BLOCKS], F32, name="m_tile")
-        g_col = g_tile[:]
-        m_col = m_tile[:]
-        with nc.allow_non_contiguous_dma(reason="one value a partition"):
-            nc.sync.dma_start(out=g_col, in_=gain[0].rearrange("(b p) -> p b", p=P))
-            nc.sync.dma_start(out=m_col, in_=miss[0].rearrange("(b p) -> p b", p=P))
 
         ident = keep.tile([P, P], F32, name="ident")
         make_identity(nc, ident[:])
 
+        w_bf = keep.tile([P, N, PACK], BF16, name="w_bf", align_bytes=64)
+        nc.vector.tensor_copy(out=w_bf[:], in_=w_raw[:].rearrange("p t n -> p n t"))
         log2inns = keep.tile([P, V], F32, name="log2inns")
         nc.scalar.activation(log2inns[:], inns_sb[:], ACT.Ln, scale=2.0)
-        w_bf = keep.tile([P, N, PACK], BF16, name="w_bf", align_bytes=64)
-        nc.scalar.copy(out=w_bf[:], in_=w_raw[:].rearrange("p t n -> p n t"))
+        late = keep.tile([P, V + 16], F32, name="late", tag="w_raw")
+        pred_sb = late[:, 0:V]
+        g_col = late[:, V : V + BLOCKS]
+        m_col = late[:, V + 8 : V + 8 + BLOCKS]
+        nc.sync.dma_start(out=pred_sb, in_=pred)
+        with nc.allow_non_contiguous_dma(reason="one value a partition"):
+            nc.sync.dma_start(out=g_col, in_=gain[0].rearrange("(b p) -> p b", p=P))
+            nc.sync.dma_start(out=m_col, in_=miss[0].rearrange("(b p) -> p b", p=P))
         sigma = keep.tile([P, V], F32, name="sigma")
         nc.scalar.activation(sigma[:], log2inns[:], ACT.Exp, scale=-0.5)
+
+        w_codes = keep.tile([P, N], U32, name="w_codes", align_bytes=64)
+        w_scales = keep.tile([P, N], U8, name="w_scales", align_bytes=64)
+        nc.vector.quantize_mx(out=w_codes[:].bitcast(FP8X4), scales=w_scales[:], in_=w_bf[:].rearrange("p n t -> p (n t)"))
 
         picked_scales = keep.tile([P, S], U8, name="picked_scales", align_bytes=64)
         for b in range(BLOCKS):
             nc.vector.tensor_copy(picked_scales[:, b * 512 : (b + 1) * 512], scales[:].indirect(offsets[:, b * 32 : (b + 1) * 32]))
-        w_codes = keep.tile([P, N], U32, name="w_codes", tag="scales", align_bytes=64)
-        w_scales = keep.tile([P, N], U8, name="w_scales", align_bytes=64)
-        nc.vector.quantize_mx(out=w_codes[:].bitcast(FP8X4), scales=w_scales[:], in_=w_bf[:].rearrange("p n t -> p (n t)"))
 
         g2 = keep.tile([P, BLOCKS], F32, name="g2")
         ng2 = keep.tile([P, BLOCKS], F32, name="ng2")
@@ -87,65 +87,97 @@ def tile_picked_ypdaf_var_p_kernel(tc, x_words, x_scales, w1, pred, inns, miss, 
         ys = []
 
         def gather(c):
-            picked = keep.tile([P, CH], U32, name=f"picked{c}", align_bytes=64)
+            picked = keep.tile([P, CH], U32, name=f"picked{c}", tag="picked", bufs=3, align_bytes=64)
             nc.vector.tensor_copy(picked[:], words[:].indirect(offsets[:, c * 16 : (c + 1) * 16]))
-            y = psum.tile([P, CH], F32, name=f"y{c}", tag="y")
+            y = psum.tile([P, CH], F32, name=f"y{c}", tag="y", bufs=3)
             nc.tensor.matmul_mx(out=y[:], lhsT=w_codes[:].bitcast(FP8X4), lhsT_scale=w_scales[:],
                                 rhs=picked[:].bitcast(FP8X4), rhs_scale=picked_scales[:, c * CH : (c + 1) * CH], start=True, stop=True)
             ys.append(y)
 
-        def innov(c):
+        def innov(c, ds=slice(0, D)):
+            b, h = divmod(c, 2)
+            nd = ds.stop - ds.start
+            nc.vector.tensor_tensor(nu[b][:, ds, h * CV : (h + 1) * CV], ys[c][:].rearrange("p (v d) -> p d v", d=D)[:, ds, :],
+                                    pred_sb[:, c * CV : (c + 1) * CV].unsqueeze(1).to_broadcast([P, nd, CV]), ALU.subtract)
+
+        def scale(c, ds=slice(0, D)):
+            b, h = divmod(c, 2)
+            nd = ds.stop - ds.start
+            cols = slice(h * CV, (h + 1) * CV)
+            nc.vector.tensor_tensor(z[b][:, ds, cols], nu[b][:, ds, cols],
+                                    sigma[:, c * CV : (c + 1) * CV].unsqueeze(1).to_broadcast([P, nd, CV]), ALU.mult)
+
+        def square(c, ds=slice(0, D)):
             b, h = divmod(c, 2)
             cols = slice(h * CV, (h + 1) * CV)
-            tr = slice(c * CV, (c + 1) * CV)
-            nc.vector.tensor_tensor(nu[b][:, :, cols], ys[c][:].rearrange("p (v d) -> p d v", d=D),
-                                    pred_sb[:, tr].unsqueeze(1).to_broadcast([P, D, CV]), ALU.subtract)
-            nc.vector.tensor_tensor(z[b][:, :, cols], nu[b][:, :, cols],
-                                    sigma[:, tr].unsqueeze(1).to_broadcast([P, D, CV]), ALU.mult)
-            nc.scalar.activation(q[b][:, :, cols], z[b][:, :, cols], ACT.Square)
-            nc.scalar.activation(lik[b][:, :, cols], q[b][:, :, cols], ACT.Exp, scale=-1.0)
+            nc.scalar.activation(q[b][:, ds, cols], z[b][:, ds, cols], ACT.Square)
 
-        def sum_over_d(src, name, b):
-            acc = psum.tile([P, P], F32, name=f"{name}{b}", tag=name)
+        def likelihood(c, ds=slice(0, D)):
+            b, h = divmod(c, 2)
+            cols = slice(h * CV, (h + 1) * CV)
+            nc.scalar.activation(lik[b][:, ds, cols], q[b][:, ds, cols], ACT.Exp, scale=-1.0)
+
+        def sum_over_d(src, name, b, acc=None):
+            if acc is None:
+                acc = psum.tile([P, P], F32, name=f"{name}{b}", tag=name)[:]
             for d in range(D):
-                nc.tensor.matmul(acc[:], src[:, d, :], ident[:], start=(d == 0), stop=(d == D - 1), is_transpose=True)
+                nc.tensor.matmul(acc, src[:, d, :], ident[:], start=(d == 0), stop=(d == D - 1), is_transpose=True)
             return acc
 
+        halves = (slice(0, 2), slice(2, 4))
         gather(0)
         gather(1)
-        innov(0)
         gather(2)
+        innov(0)
         innov(1)
+        scale(0)
+        square(0)
+        likelihood(0)
         gather(3)
+        scale(1)
+        square(1)
+        likelihood(1)
         innov(2)
+        scale(2)
+        square(2)
         innov(3)
-        z0 = [sum_over_d(lik[b], "z0_", b) for b in range(BLOCKS)]
+        for ds in halves:
+            scale(3, ds)
+        square(3, halves[0])
+        likelihood(2)
+        square(3, halves[1])
+        for ds in halves:
+            likelihood(3, ds)
+        z0_bank = psum.tile([P, V], F32, name="z0_bank", bufs=1)
+        z0 = [sum_over_d(lik[b], "z0_", b, z0_bank[:, b * P : (b + 1) * P]) for b in range(BLOCKS)]
         z1, z2 = [], []
         for b in range(BLOCKS):
-            for dd in range(0, D, 2):
-                nc.vector.tensor_tensor(e2[b][:, dd : dd + 2, :], lik[b][:, dd : dd + 2, :], q[b][:, dd : dd + 2, :], ALU.mult)
+            parts = halves if b else (slice(0, D),)
+            for ds in parts:
+                nc.vector.tensor_tensor(e2[b][:, ds, :], lik[b][:, ds, :], q[b][:, ds, :], ALU.mult)
             z2.append(sum_over_d(e2[b], "z2_", b))
-            for dd in range(0, D, 2):
-                nc.vector.tensor_tensor(e1[b][:, dd : dd + 2, :], lik[b][:, dd : dd + 2, :], z[b][:, dd : dd + 2, :], ALU.mult)
+            for ds in parts:
+                nc.vector.tensor_tensor(e1[b][:, ds, :], lik[b][:, ds, :], z[b][:, ds, :], ALU.mult)
             z1.append(sum_over_d(e1[b], "z1_", b))
 
+        def squares(name):
+            return [keep.tile([P, P], F32, name=f"{name}{b}") for b in range(BLOCKS)]
+
+        rho, r, k3, k, c1, c2, res = (squares(n) for n in ("rho", "r", "k3", "k", "c1", "c2", "res"))
         for b in range(BLOCKS):
-            col = slice(b, b + 1)
-            rho = keep.tile([P, P], F32, name=f"rho{b}")
-            nc.scalar.activation(rho[:], z0[b][:], ACT.Abs_reciprocal_sqrt, bias=m_col[:, col])
-            r = keep.tile([P, P], F32, name=f"r{b}")
-            nc.scalar.activation(r[:], rho[:], ACT.Square)
-            k3 = keep.tile([P, P], F32, name=f"k3{b}")
-            nc.scalar.activation(k3[:], r[:], ACT.Identity, scale=gm[:, col], bias=omg[:, col])
-            k = keep.tile([P, P], F32, name=f"k{b}")
-            nc.vector.scalar_tensor_tensor(k[:], z2[b][:], g2[:, col], r[:], ALU.mult, ALU.mult)
-            c1 = keep.tile([P, P], F32, name=f"c1{b}")
-            nc.vector.tensor_tensor(c1[:], z1[b][:], r[:], ALU.mult)
-            c2 = keep.tile([P, P], F32, name=f"c2{b}")
-            nc.vector.scalar_tensor_tensor(c2[:], c1[:], ng2[:, col], c1[:], ALU.mult, ALU.mult)
-            back = psum.tile([P, CH], F32, name=f"back{b}", tag="y")
+            nc.scalar.activation(rho[b][:], z0[b], ACT.Abs_reciprocal_sqrt, bias=m_col[:, b : b + 1])
+        for b in range(BLOCKS):
+            nc.scalar.activation(r[b][:], rho[b][:], ACT.Square)
+        for b in range(BLOCKS):
+            nc.scalar.activation(k3[b][:], r[b][:], ACT.Identity, scale=gm[:, b : b + 1], bias=omg[:, b : b + 1])
+        for b in range(BLOCKS):
+            nc.vector.tensor_tensor(c1[b][:], z1[b], r[b][:], ALU.mult)
+            nc.vector.scalar_tensor_tensor(k[b][:], z2[b], g2[:, b : b + 1], r[b][:], ALU.mult, ALU.mult)
+        for b in range(BLOCKS):
+            nc.vector.scalar_tensor_tensor(c2[b][:], c1[b][:], ng2[:, b : b + 1], c1[b][:], ALU.mult, ALU.mult)
+        for b in range(BLOCKS):
+            back = psum.tile([P, CH], F32, name=f"back{b}", tag="y", bufs=3)
             for i, term in enumerate((k3, k, c2)):
-                nc.tensor.matmul(back[:, 0:P], term[:], ident[:], start=(i == 0), stop=(i == 2), is_transpose=True)
-            res = keep.tile([P, P], F32, name=f"res{b}")
-            nc.vector.tensor_tensor(res[:], back[:, 0:P], inns_sb[:, b * P : (b + 1) * P], ALU.mult)
-            nc.sync.dma_start(out=out[:, b * P : (b + 1) * P], in_=res[:])
+                nc.tensor.matmul(back[:, 0:P], term[b][:], ident[:], start=(i == 0), stop=(i == 2), is_transpose=True)
+            nc.vector.tensor_tensor(res[b][:], back[:, 0:P], inns_sb[:, b * P : (b + 1) * P], ALU.mult)
+            nc.sync.dma_start(out=out[:, b * P : (b + 1) * P], in_=res[b][:])

@@ -19,19 +19,25 @@ ALU = mybir.AluOpType
 P = 128
 PACK = 4
 BLOCKS = V // P
-CH = 256
-CV = CH // D
+CHUNK = 256
+CHUNK_TRACKS = CHUNK // D
+CHUNKS_PER_BLOCK = P // CHUNK_TRACKS
+PER_COLUMN = 16
+PRODUCT_BANKS = 3
+PAD = 8
 
 
 def tile_picked_ypdaf_var_p_kernel(tc, x_words, x_scales, w1, pred, inns, miss, gain, offs, out):
     nc = tc.nc
     with ExitStack() as ctx:
         keep = ctx.enter_context(tc.tile_pool(name="keep", bufs=1))
-        psum = ctx.enter_context(tc.psum_pool(name="psum", bufs=2))
+        psum = ctx.enter_context(tc.psum_pool(name="psum", bufs=BLOCKS))
 
-        offsets = keep.tile([P, S // 16], U16, name="offsets")
+        def per_block(name, shape):
+            return [keep.tile(shape, F32, name=f"{name}{b}") for b in range(BLOCKS)]
+
+        offsets = keep.tile([P, S // PER_COLUMN], U16, name="offsets")
         nc.sync.dma_start(offsets[:], offs)
-
         w_raw = keep.tile([P, PACK, N], F32, name="w_raw", tag="w_raw")
         nc.sync.dma_start(out=w_raw[:], in_=w1.rearrange("(p t) n -> p t n", t=PACK))
         inns_sb = keep.tile([P, V], F32, name="inns_sb")
@@ -39,7 +45,10 @@ def tile_picked_ypdaf_var_p_kernel(tc, x_words, x_scales, w1, pred, inns, miss, 
         scales = keep.tile([P, T], U8, name="scales", align_bytes=64)
         nc.vector.memset(scales[:].bitcast(I32), 0)
         for quad in range(4):
-            nc.sync.dma_start(out=scales[32 * quad : 32 * quad + 4, :].bitcast(I32), in_=x_scales[0, 4 * quad : 4 * quad + 4, :].bitcast(I32))
+            nc.sync.dma_start(
+                out=scales[32 * quad : 32 * quad + 4, :].bitcast(I32),
+                in_=x_scales[0, 4 * quad : 4 * quad + 4, :].bitcast(I32),
+            )
         words = keep.tile([P, T], U32, name="words", align_bytes=64)
         nc.sync.dma_start(out=words[:].bitcast(I32), in_=x_words[0].rearrange("p c t -> p (c t)").bitcast(I32))
 
@@ -48,136 +57,133 @@ def tile_picked_ypdaf_var_p_kernel(tc, x_words, x_scales, w1, pred, inns, miss, 
 
         w_bf = keep.tile([P, N, PACK], BF16, name="w_bf", align_bytes=64)
         nc.vector.tensor_copy(out=w_bf[:], in_=w_raw[:].rearrange("p t n -> p n t"))
-        log2inns = keep.tile([P, V], F32, name="log2inns")
-        nc.scalar.activation(log2inns[:], inns_sb[:], ACT.Ln, scale=2.0)
-        late = keep.tile([P, V + 16], F32, name="late", tag="w_raw")
+        log_var = keep.tile([P, V], F32, name="log_var")
+        nc.scalar.activation(log_var[:], inns_sb[:], ACT.Ln, scale=2.0)
+
+        late = keep.tile([P, V + 2 * PAD], F32, name="late", tag="w_raw")
         pred_sb = late[:, 0:V]
         g_col = late[:, V : V + BLOCKS]
-        m_col = late[:, V + 8 : V + 8 + BLOCKS]
+        miss_col = late[:, V + PAD : V + PAD + BLOCKS]
         nc.sync.dma_start(out=pred_sb, in_=pred)
-        with nc.allow_non_contiguous_dma(reason="one value a partition"):
+        with nc.allow_non_contiguous_dma(reason="one value a partition and block"):
             nc.sync.dma_start(out=g_col, in_=gain[0].rearrange("(b p) -> p b", p=P))
-            nc.sync.dma_start(out=m_col, in_=miss[0].rearrange("(b p) -> p b", p=P))
+            nc.sync.dma_start(out=miss_col, in_=miss[0].rearrange("(b p) -> p b", p=P))
+
         sigma = keep.tile([P, V], F32, name="sigma")
-        nc.scalar.activation(sigma[:], log2inns[:], ACT.Exp, scale=-0.5)
+        nc.scalar.activation(sigma[:], log_var[:], ACT.Exp, scale=-0.5)
 
         w_codes = keep.tile([P, N], U32, name="w_codes", align_bytes=64)
         w_scales = keep.tile([P, N], U8, name="w_scales", align_bytes=64)
-        nc.vector.quantize_mx(out=w_codes[:].bitcast(FP8X4), scales=w_scales[:], in_=w_bf[:].rearrange("p n t -> p (n t)"))
-
+        nc.vector.quantize_mx(
+            out=w_codes[:].bitcast(FP8X4), scales=w_scales[:], in_=w_bf[:].rearrange("p n t -> p (n t)")
+        )
         picked_scales = keep.tile([P, S], U8, name="picked_scales", align_bytes=64)
+        nc.vector.tensor_copy(picked_scales[:], scales[:].indirect(offsets[:]))
+
+        root2_g = keep.tile([P, BLOCKS], F32, name="root2_g")
+        minus_g = keep.tile([P, BLOCKS], F32, name="minus_g")
+        g_minus_1 = keep.tile([P, BLOCKS], F32, name="g_minus_1")
+        minus_g_miss = keep.tile([P, BLOCKS], F32, name="minus_g_miss")
+        minus_gg = keep.tile([P, BLOCKS], F32, name="minus_gg")
+        minus_2gg = keep.tile([P, BLOCKS], F32, name="minus_2gg")
+        nc.scalar.activation(minus_g[:], g_col, ACT.Copy, scale=-1.0)
+        nc.scalar.activation(root2_g[:], g_col, ACT.Copy, scale=2.0**0.5)
+        nc.scalar.activation(g_minus_1[:], g_col, ACT.Identity, bias=-1.0)
         for b in range(BLOCKS):
-            nc.vector.tensor_copy(picked_scales[:, b * 512 : (b + 1) * 512], scales[:].indirect(offsets[:, b * 32 : (b + 1) * 32]))
+            col = slice(b, b + 1)
+            nc.scalar.activation(minus_g_miss[:, col], miss_col[:, col], ACT.Copy, scale=minus_g[:, col])
+            nc.scalar.activation(minus_gg[:, col], g_col[:, col], ACT.Copy, scale=minus_g[:, col])
+        nc.scalar.activation(minus_2gg[:], minus_gg[:], ACT.Copy, scale=2.0)
 
-        g2 = keep.tile([P, BLOCKS], F32, name="g2")
-        ng2 = keep.tile([P, BLOCKS], F32, name="ng2")
-        gm = keep.tile([P, BLOCKS], F32, name="gm")
-        omg = keep.tile([P, BLOCKS], F32, name="omg")
-        nc.scalar.activation(g2[:], g_col, ACT.Square, scale=2.0**0.5)
-        nc.scalar.activation(ng2[:], g2[:], ACT.Copy, scale=-1.0)
-        nc.scalar.activation(omg[:], g_col, ACT.Identity, scale=-1.0, bias=1.0)
+        def product(c):
+            picked = keep.tile([P, CHUNK], U32, name=f"picked{c}", align_bytes=64)
+            cols = CHUNK // PER_COLUMN
+            nc.vector.tensor_copy(picked[:], words[:].indirect(offsets[:, c * cols : (c + 1) * cols]))
+            y = psum.tile([P, CHUNK], F32, name=f"y{c}", tag="product", bufs=PRODUCT_BANKS)
+            nc.tensor.matmul_mx(
+                out=y[:],
+                lhsT=w_codes[:].bitcast(FP8X4),
+                lhsT_scale=w_scales[:],
+                rhs=picked[:].bitcast(FP8X4),
+                rhs_scale=picked_scales[:, c * CHUNK : (c + 1) * CHUNK],
+                start=True,
+                stop=True,
+            )
+            return y
+
+        def chunk_of(tiles, c):
+            b, part = divmod(c, CHUNKS_PER_BLOCK)
+            return tiles[b][:, :, part * CHUNK_TRACKS : (part + 1) * CHUNK_TRACKS]
+
+        def over_d(row, c):
+            tracks = row[:, c * CHUNK_TRACKS : (c + 1) * CHUNK_TRACKS]
+            return tracks.unsqueeze(1).to_broadcast([P, D, CHUNK_TRACKS])
+
+        def add_transposed(acc, squares):
+            for i, square in enumerate(squares):
+                nc.tensor.matmul(acc, square, ident[:], start=(i == 0), stop=(i == len(squares) - 1), is_transpose=True)
+
+        nu, z, zz, lik, lik_z, lik_zz = (
+            per_block(name, [P, D, P]) for name in ("nu", "z", "zz", "lik", "lik_z", "lik_zz")
+        )
+
+        ys = [product(c) for c in range(PRODUCT_BANKS)]
         for b in range(BLOCKS):
-            nc.scalar.activation(gm[:, b : b + 1], m_col[:, b : b + 1], ACT.Copy, scale=g_col[:, b : b + 1])
+            chunks = range(b * CHUNKS_PER_BLOCK, (b + 1) * CHUNKS_PER_BLOCK)
+            for c in chunks:
+                nc.vector.tensor_tensor(
+                    chunk_of(nu, c), ys[c][:].rearrange("p (v d) -> p d v", d=D), over_d(pred_sb, c), ALU.subtract
+                )
+                if c == 0:
+                    ys.append(product(PRODUCT_BANKS))
+            for c in chunks:
+                nc.vector.tensor_tensor(chunk_of(z, c), chunk_of(nu, c), over_d(sigma[:], c), ALU.mult)
+            for c in chunks:
+                nc.scalar.activation(chunk_of(zz, c), chunk_of(z, c), ACT.Square)
+            for c in chunks:
+                nc.scalar.activation(chunk_of(lik, c), chunk_of(zz, c), ACT.Exp, scale=-1.0)
 
-        def block_tiles(name):
-            return [keep.tile([P, D, P], F32, name=f"{name}{b}") for b in range(BLOCKS)]
-
-        nu, z, q, lik, e1, e2 = (block_tiles(n) for n in ("nu", "z", "q", "lik", "e1", "e2"))
-
-        ys = []
-
-        def gather(c):
-            picked = keep.tile([P, CH], U32, name=f"picked{c}", tag="picked", bufs=3, align_bytes=64)
-            nc.vector.tensor_copy(picked[:], words[:].indirect(offsets[:, c * 16 : (c + 1) * 16]))
-            y = psum.tile([P, CH], F32, name=f"y{c}", tag="y", bufs=3)
-            nc.tensor.matmul_mx(out=y[:], lhsT=w_codes[:].bitcast(FP8X4), lhsT_scale=w_scales[:],
-                                rhs=picked[:].bitcast(FP8X4), rhs_scale=picked_scales[:, c * CH : (c + 1) * CH], start=True, stop=True)
-            ys.append(y)
-
-        def innov(c, ds=slice(0, D)):
-            b, h = divmod(c, 2)
-            nd = ds.stop - ds.start
-            nc.vector.tensor_tensor(nu[b][:, ds, h * CV : (h + 1) * CV], ys[c][:].rearrange("p (v d) -> p d v", d=D)[:, ds, :],
-                                    pred_sb[:, c * CV : (c + 1) * CV].unsqueeze(1).to_broadcast([P, nd, CV]), ALU.subtract)
-
-        def scale(c, ds=slice(0, D)):
-            b, h = divmod(c, 2)
-            nd = ds.stop - ds.start
-            cols = slice(h * CV, (h + 1) * CV)
-            nc.vector.tensor_tensor(z[b][:, ds, cols], nu[b][:, ds, cols],
-                                    sigma[:, c * CV : (c + 1) * CV].unsqueeze(1).to_broadcast([P, nd, CV]), ALU.mult)
-
-        def square(c, ds=slice(0, D)):
-            b, h = divmod(c, 2)
-            cols = slice(h * CV, (h + 1) * CV)
-            nc.scalar.activation(q[b][:, ds, cols], z[b][:, ds, cols], ACT.Square)
-
-        def likelihood(c, ds=slice(0, D)):
-            b, h = divmod(c, 2)
-            cols = slice(h * CV, (h + 1) * CV)
-            nc.scalar.activation(lik[b][:, ds, cols], q[b][:, ds, cols], ACT.Exp, scale=-1.0)
-
-        def sum_over_d(src, name, b, acc=None):
-            if acc is None:
-                acc = psum.tile([P, P], F32, name=f"{name}{b}", tag=name)[:]
-            for d in range(D):
-                nc.tensor.matmul(acc, src[:, d, :], ident[:], start=(d == 0), stop=(d == D - 1), is_transpose=True)
-            return acc
-
-        halves = (slice(0, 2), slice(2, 4))
-        gather(0)
-        gather(1)
-        gather(2)
-        innov(0)
-        innov(1)
-        scale(0)
-        square(0)
-        likelihood(0)
-        gather(3)
-        scale(1)
-        square(1)
-        likelihood(1)
-        innov(2)
-        scale(2)
-        square(2)
-        innov(3)
-        for ds in halves:
-            scale(3, ds)
-        square(3, halves[0])
-        likelihood(2)
-        square(3, halves[1])
-        for ds in halves:
-            likelihood(3, ds)
-        z0_bank = psum.tile([P, V], F32, name="z0_bank", bufs=1)
-        z0 = [sum_over_d(lik[b], "z0_", b, z0_bank[:, b * P : (b + 1) * P]) for b in range(BLOCKS)]
-        z1, z2 = [], []
+        s0_bank = psum.tile([P, V], F32, name="s0_bank", bufs=1)
+        s0 = [s0_bank[:, b * P : (b + 1) * P] for b in range(BLOCKS)]
+        s1 = [psum.tile([P, P], F32, name=f"s1_{b}", tag="s1") for b in range(BLOCKS)]
+        s2 = [psum.tile([P, P], F32, name=f"s2_{b}", tag="s2") for b in range(BLOCKS)]
+        halves = (slice(0, D // 2), slice(D // 2, D))
+        lik_pairs = keep.tile([P, D // 2, P], F32, name="lik_pairs")
         for b in range(BLOCKS):
-            parts = halves if b else (slice(0, D),)
-            for ds in parts:
-                nc.vector.tensor_tensor(e2[b][:, ds, :], lik[b][:, ds, :], q[b][:, ds, :], ALU.mult)
-            z2.append(sum_over_d(e2[b], "z2_", b))
-            for ds in parts:
-                nc.vector.tensor_tensor(e1[b][:, ds, :], lik[b][:, ds, :], z[b][:, ds, :], ALU.mult)
-            z1.append(sum_over_d(e1[b], "z1_", b))
+            if b == BLOCKS - 1:
+                nc.vector.tensor_tensor(lik_pairs[:], lik[b][:, halves[0], :], lik[b][:, halves[1], :], ALU.add)
+                add_transposed(s0[b], [lik_pairs[:, i, :] for i in range(D // 2)])
+            else:
+                add_transposed(s0[b], [lik[b][:, d, :] for d in range(D)])
+            for product_tile, factor, total in ((lik_z, z, s1), (lik_zz, zz, s2)):
+                for half in halves:
+                    nc.vector.tensor_tensor(
+                        product_tile[b][:, half, :], lik[b][:, half, :], factor[b][:, half, :], ALU.mult
+                    )
+                add_transposed(total[b][:], [product_tile[b][:, d, :] for d in range(D)])
 
-        def squares(name):
-            return [keep.tile([P, P], F32, name=f"{name}{b}") for b in range(BLOCKS)]
-
-        rho, r, k3, k, c1, c2, res = (squares(n) for n in ("rho", "r", "k3", "k", "c1", "c2", "res"))
+        root_r, r, miss_term, mean, s2_term, mean_term, result = (
+            per_block(name, [P, P]) for name in ("root_r", "r", "miss_term", "mean", "s2_term", "mean_term", "result")
+        )
+        cols = [slice(b, b + 1) for b in range(BLOCKS)]
         for b in range(BLOCKS):
-            nc.scalar.activation(rho[b][:], z0[b], ACT.Abs_reciprocal_sqrt, bias=m_col[:, b : b + 1])
+            nc.scalar.activation(root_r[b][:], s0[b], ACT.Abs_reciprocal_sqrt, bias=miss_col[:, cols[b]])
         for b in range(BLOCKS):
-            nc.scalar.activation(r[b][:], rho[b][:], ACT.Square)
+            nc.scalar.activation(r[b][:], root_r[b][:], ACT.Square)
         for b in range(BLOCKS):
-            nc.scalar.activation(k3[b][:], r[b][:], ACT.Identity, scale=gm[:, b : b + 1], bias=omg[:, b : b + 1])
+            nc.scalar.activation(
+                miss_term[b][:], r[b][:], ACT.Identity, scale=minus_g_miss[:, cols[b]], bias=g_minus_1[:, cols[b]]
+            )
         for b in range(BLOCKS):
-            nc.vector.tensor_tensor(c1[b][:], z1[b], r[b][:], ALU.mult)
-            nc.vector.scalar_tensor_tensor(k[b][:], z2[b], g2[:, b : b + 1], r[b][:], ALU.mult, ALU.mult)
+            nc.vector.tensor_tensor(mean[b][:], s1[b][:], r[b][:], ALU.mult)
         for b in range(BLOCKS):
-            nc.vector.scalar_tensor_tensor(c2[b][:], c1[b][:], ng2[:, b : b + 1], c1[b][:], ALU.mult, ALU.mult)
+            nc.vector.scalar_tensor_tensor(s2_term[b][:], s2[b][:], minus_2gg[:, cols[b]], r[b][:], ALU.mult, ALU.mult)
         for b in range(BLOCKS):
-            back = psum.tile([P, CH], F32, name=f"back{b}", tag="y", bufs=3)
-            for i, term in enumerate((k3, k, c2)):
-                nc.tensor.matmul(back[:, 0:P], term[b][:], ident[:], start=(i == 0), stop=(i == 2), is_transpose=True)
-            nc.vector.tensor_tensor(res[b][:], back[:, 0:P], inns_sb[:, b * P : (b + 1) * P], ALU.mult)
-            nc.sync.dma_start(out=out[:, b * P : (b + 1) * P], in_=res[b][:])
+            nc.scalar.activation(mean_term[b][:], mean[b][:], ACT.Square, scale=root2_g[:, cols[b]])
+        for b in range(BLOCKS):
+            tracks = slice(b * P, (b + 1) * P)
+            bank = psum.tile([P, CHUNK], F32, name=f"minus_bracket{b}", tag="product", bufs=PRODUCT_BANKS)
+            minus_bracket = bank[:, 0:P]
+            add_transposed(minus_bracket, [miss_term[b][:], s2_term[b][:], mean_term[b][:]])
+            nc.vector.scalar_tensor_tensor(result[b][:], minus_bracket, -1.0, inns_sb[:, tracks], ALU.mult, ALU.mult)
+            nc.sync.dma_start(out=out[:, tracks], in_=result[b][:])

from contextlib import ExitStack

import concourse.mybir as mybir
from concourse.masks import make_identity

K, T, S, D, N, V = 512, 2048, 1024, 4, 128, 256
FLOPS = 2 * K * N * S

F32 = mybir.dt.float32
BF16 = mybir.dt.bfloat16
I32 = mybir.dt.int32
U32 = mybir.dt.uint32
U16 = mybir.dt.uint16
U8 = mybir.dt.uint8
FP8X4 = mybir.dt.float8_e4m3fn_x4
ACT = mybir.ActivationFunctionType
ALU = mybir.AluOpType

P = 128
PACK = 4
BLOCKS = V // P
CHUNK = 256
CHUNK_TRACKS = CHUNK // D
CHUNKS_PER_BLOCK = P // CHUNK_TRACKS
PER_COLUMN = 16
PRODUCT_BANKS = 3
PAD = 8


def tile_picked_ypdaf_var_p_kernel(tc, x_words, x_scales, w1, pred, inns, miss, gain, offs, out):
    nc = tc.nc
    with ExitStack() as ctx:
        keep = ctx.enter_context(tc.tile_pool(name="keep", bufs=1))
        psum = ctx.enter_context(tc.psum_pool(name="psum", bufs=BLOCKS))

        def per_block(name, shape):
            return [keep.tile(shape, F32, name=f"{name}{b}") for b in range(BLOCKS)]

        offsets = keep.tile([P, S // PER_COLUMN], U16, name="offsets")
        nc.sync.dma_start(offsets[:], offs)
        w_raw = keep.tile([P, PACK, N], F32, name="w_raw", tag="w_raw")
        nc.sync.dma_start(out=w_raw[:], in_=w1.rearrange("(p t) n -> p t n", t=PACK))
        inns_sb = keep.tile([P, V], F32, name="inns_sb")
        nc.sync.dma_start(out=inns_sb[:], in_=inns)
        scales = keep.tile([P, T], U8, name="scales", align_bytes=64)
        nc.vector.memset(scales[:].bitcast(I32), 0)
        for quad in range(4):
            nc.sync.dma_start(
                out=scales[32 * quad : 32 * quad + 4, :].bitcast(I32),
                in_=x_scales[0, 4 * quad : 4 * quad + 4, :].bitcast(I32),
            )
        words = keep.tile([P, T], U32, name="words", align_bytes=64)
        nc.sync.dma_start(out=words[:].bitcast(I32), in_=x_words[0].rearrange("p c t -> p (c t)").bitcast(I32))

        ident = keep.tile([P, P], F32, name="ident")
        make_identity(nc, ident[:])

        w_bf = keep.tile([P, N, PACK], BF16, name="w_bf", align_bytes=64)
        nc.vector.tensor_copy(out=w_bf[:], in_=w_raw[:].rearrange("p t n -> p n t"))
        log_var = keep.tile([P, V], F32, name="log_var")
        nc.scalar.activation(log_var[:], inns_sb[:], ACT.Ln, scale=2.0)

        late = keep.tile([P, V + 2 * PAD], F32, name="late", tag="w_raw")
        pred_sb = late[:, 0:V]
        g_col = late[:, V : V + BLOCKS]
        miss_col = late[:, V + PAD : V + PAD + BLOCKS]
        nc.sync.dma_start(out=pred_sb, in_=pred)
        with nc.allow_non_contiguous_dma(reason="one value a partition and block"):
            nc.sync.dma_start(out=g_col, in_=gain[0].rearrange("(b p) -> p b", p=P))
            nc.sync.dma_start(out=miss_col, in_=miss[0].rearrange("(b p) -> p b", p=P))

        sigma = keep.tile([P, V], F32, name="sigma")
        nc.scalar.activation(sigma[:], log_var[:], ACT.Exp, scale=-0.5)

        w_codes = keep.tile([P, N], U32, name="w_codes", align_bytes=64)
        w_scales = keep.tile([P, N], U8, name="w_scales", align_bytes=64)
        nc.vector.quantize_mx(
            out=w_codes[:].bitcast(FP8X4), scales=w_scales[:], in_=w_bf[:].rearrange("p n t -> p (n t)")
        )
        picked_scales = keep.tile([P, S], U8, name="picked_scales", align_bytes=64)
        nc.vector.tensor_copy(picked_scales[:], scales[:].indirect(offsets[:]))

        root2_g = keep.tile([P, BLOCKS], F32, name="root2_g")
        minus_g = keep.tile([P, BLOCKS], F32, name="minus_g")
        g_minus_1 = keep.tile([P, BLOCKS], F32, name="g_minus_1")
        minus_g_miss = keep.tile([P, BLOCKS], F32, name="minus_g_miss")
        minus_gg = keep.tile([P, BLOCKS], F32, name="minus_gg")
        minus_2gg = keep.tile([P, BLOCKS], F32, name="minus_2gg")
        nc.scalar.activation(minus_g[:], g_col, ACT.Copy, scale=-1.0)
        nc.scalar.activation(root2_g[:], g_col, ACT.Copy, scale=2.0**0.5)
        nc.scalar.activation(g_minus_1[:], g_col, ACT.Identity, bias=-1.0)
        for b in range(BLOCKS):
            col = slice(b, b + 1)
            nc.scalar.activation(minus_g_miss[:, col], miss_col[:, col], ACT.Copy, scale=minus_g[:, col])
            nc.scalar.activation(minus_gg[:, col], g_col[:, col], ACT.Copy, scale=minus_g[:, col])
        nc.scalar.activation(minus_2gg[:], minus_gg[:], ACT.Copy, scale=2.0)

        def product(c):
            picked = keep.tile([P, CHUNK], U32, name=f"picked{c}", align_bytes=64)
            cols = CHUNK // PER_COLUMN
            nc.vector.tensor_copy(picked[:], words[:].indirect(offsets[:, c * cols : (c + 1) * cols]))
            y = psum.tile([P, CHUNK], F32, name=f"y{c}", tag="product", bufs=PRODUCT_BANKS)
            nc.tensor.matmul_mx(
                out=y[:],
                lhsT=w_codes[:].bitcast(FP8X4),
                lhsT_scale=w_scales[:],
                rhs=picked[:].bitcast(FP8X4),
                rhs_scale=picked_scales[:, c * CHUNK : (c + 1) * CHUNK],
                start=True,
                stop=True,
            )
            return y

        def chunk_of(tiles, c):
            b, part = divmod(c, CHUNKS_PER_BLOCK)
            return tiles[b][:, :, part * CHUNK_TRACKS : (part + 1) * CHUNK_TRACKS]

        def over_d(row, c):
            tracks = row[:, c * CHUNK_TRACKS : (c + 1) * CHUNK_TRACKS]
            return tracks.unsqueeze(1).to_broadcast([P, D, CHUNK_TRACKS])

        def add_transposed(acc, squares):
            for i, square in enumerate(squares):
                nc.tensor.matmul(acc, square, ident[:], start=(i == 0), stop=(i == len(squares) - 1), is_transpose=True)

        nu, z, zz, lik, lik_z, lik_zz = (
            per_block(name, [P, D, P]) for name in ("nu", "z", "zz", "lik", "lik_z", "lik_zz")
        )

        ys = [product(c) for c in range(PRODUCT_BANKS)]
        for b in range(BLOCKS):
            chunks = range(b * CHUNKS_PER_BLOCK, (b + 1) * CHUNKS_PER_BLOCK)
            for c in chunks:
                nc.vector.tensor_tensor(
                    chunk_of(nu, c), ys[c][:].rearrange("p (v d) -> p d v", d=D), over_d(pred_sb, c), ALU.subtract
                )
                if c == 0:
                    ys.append(product(PRODUCT_BANKS))
            for c in chunks:
                nc.vector.tensor_tensor(chunk_of(z, c), chunk_of(nu, c), over_d(sigma[:], c), ALU.mult)
            for c in chunks:
                nc.scalar.activation(chunk_of(zz, c), chunk_of(z, c), ACT.Square)
            for c in chunks:
                nc.scalar.activation(chunk_of(lik, c), chunk_of(zz, c), ACT.Exp, scale=-1.0)

        s0_bank = psum.tile([P, V], F32, name="s0_bank", bufs=1)
        s0 = [s0_bank[:, b * P : (b + 1) * P] for b in range(BLOCKS)]
        s1 = [psum.tile([P, P], F32, name=f"s1_{b}", tag="s1") for b in range(BLOCKS)]
        s2 = [psum.tile([P, P], F32, name=f"s2_{b}", tag="s2") for b in range(BLOCKS)]
        halves = (slice(0, D // 2), slice(D // 2, D))
        lik_pairs = keep.tile([P, D // 2, P], F32, name="lik_pairs")
        for b in range(BLOCKS):
            if b == BLOCKS - 1:
                nc.vector.tensor_tensor(lik_pairs[:], lik[b][:, halves[0], :], lik[b][:, halves[1], :], ALU.add)
                add_transposed(s0[b], [lik_pairs[:, i, :] for i in range(D // 2)])
            else:
                add_transposed(s0[b], [lik[b][:, d, :] for d in range(D)])
            for product_tile, factor, total in ((lik_z, z, s1), (lik_zz, zz, s2)):
                for half in halves:
                    nc.vector.tensor_tensor(
                        product_tile[b][:, half, :], lik[b][:, half, :], factor[b][:, half, :], ALU.mult
                    )
                add_transposed(total[b][:], [product_tile[b][:, d, :] for d in range(D)])

        root_r, r, miss_term, mean, s2_term, mean_term, result = (
            per_block(name, [P, P]) for name in ("root_r", "r", "miss_term", "mean", "s2_term", "mean_term", "result")
        )
        cols = [slice(b, b + 1) for b in range(BLOCKS)]
        for b in range(BLOCKS):
            nc.scalar.activation(root_r[b][:], s0[b], ACT.Abs_reciprocal_sqrt, bias=miss_col[:, cols[b]])
        for b in range(BLOCKS):
            nc.scalar.activation(r[b][:], root_r[b][:], ACT.Square)
        for b in range(BLOCKS):
            nc.scalar.activation(
                miss_term[b][:], r[b][:], ACT.Identity, scale=minus_g_miss[:, cols[b]], bias=g_minus_1[:, cols[b]]
            )
        for b in range(BLOCKS):
            nc.vector.tensor_tensor(mean[b][:], s1[b][:], r[b][:], ALU.mult)
        for b in range(BLOCKS):
            nc.vector.scalar_tensor_tensor(s2_term[b][:], s2[b][:], minus_2gg[:, cols[b]], r[b][:], ALU.mult, ALU.mult)
        for b in range(BLOCKS):
            nc.scalar.activation(mean_term[b][:], mean[b][:], ACT.Square, scale=root2_g[:, cols[b]])
        for b in range(BLOCKS):
            tracks = slice(b * P, (b + 1) * P)
            bank = psum.tile([P, CHUNK], F32, name=f"minus_bracket{b}", tag="product", bufs=PRODUCT_BANKS)
            minus_bracket = bank[:, 0:P]
            add_transposed(minus_bracket, [miss_term[b][:], s2_term[b][:], mean_term[b][:]])
            nc.vector.scalar_tensor_tensor(result[b][:], minus_bracket, -1.0, inns_sb[:, tracks], ALU.mult, ALU.mult)
            nc.sync.dma_start(out=out[:, tracks], in_=result[b][:])
